import numpy as np
import ml_dtypes


def mxq(x, axis, fmt="e4m3"):
    dtype, down = {"e4m3": (ml_dtypes.float8_e4m3fn, 7), "e5m2": (ml_dtypes.float8_e5m2, 14)}[fmt]
    v = np.moveaxis(np.asarray(x, np.float32).astype(ml_dtypes.bfloat16).astype(np.float64), axis, -1)
    blocks = v.reshape(v.shape[:-1] + (-1, 32))
    amax = np.abs(blocks).max(-1, keepdims=True)
    byte = np.maximum(np.where(amax > 0, np.frexp(amax)[1] - 1 + 127, 0) - down, 1)
    scale = np.exp2(byte - 127.0)
    codes = (blocks / scale).astype(np.float32).astype(dtype).astype(np.float64)
    return np.moveaxis((codes * scale).reshape(v.shape), -1, axis)


WIDE = False


def mx_kscale(k):
    if not WIDE:
        return np.ones(k)
    levels = np.array([24, -24, 12, -12, 0])
    if k % 512:
        return np.exp2(np.random.permutation(np.resize(levels, k // 32))).repeat(32)
    a = np.empty((k // 512, 16))
    for p in range(k // 512):
        a[p, :8] = np.random.permutation(np.resize(levels, 8))
        for g in range(8):
            far = levels[np.abs(levels - a[p, g]) >= 10]
            a[p, g + 8] = far[np.random.randint(len(far))]
    return np.exp2(a.ravel()).repeat(32)


def f64(x):
    return np.asarray(x).astype(np.float64)


E2M1 = np.array([0.0, 0.5, 1.0, 1.5, 2.0, 3.0, 4.0, 6.0, -0.0, -0.5, -1.0, -1.5, -2.0, -3.0, -4.0, -6.0])


def pack_weight(w, fmt):
    k, n = w.shape
    w = f64(np.asarray(w, np.float32).astype(ml_dtypes.bfloat16)).reshape(k // 32, 32, n)
    amax = np.abs(w).max(1)
    if fmt == "e4m3":
        byte = np.frexp(amax)[1] - 1 + 127 - 7
    else:
        mant, ex = np.frexp(amax / 6.0)
        byte = np.where(mant > 0.5, ex, ex - 1) + 127
    byte = np.clip(np.where(amax > 0, byte, 1), 1, 254)
    scaled = (w * np.exp2(127.0 - byte)[:, None, :]).reshape(k, n).astype(np.float32)
    by_word = np.ascontiguousarray(scaled.reshape(k // 512, 128, 4, n).transpose(0, 1, 3, 2))
    if fmt == "e4m3":
        words = by_word.astype(ml_dtypes.float8_e4m3fn).view(np.uint8)
    else:
        c = by_word.astype(ml_dtypes.float4_e2m1fn).view(np.uint8) & 0xF
        words = (c[..., 0::2] | (c[..., 1::2] << 4)).reshape(k // 512, 128, 2 * n)
    return np.ascontiguousarray(words), np.ascontiguousarray(byte.astype(np.uint8).reshape(k // 512, 16, n))


def unpack_weight(words, scales, fmt):
    g, _, n = scales.shape
    words = np.ascontiguousarray(words).reshape(g, 128, n, -1)
    if fmt == "e4m3":
        vals = words.view(ml_dtypes.float8_e4m3fn).astype(np.float64)
    else:
        nib = np.empty((g, 128, n, 4), np.uint8)
        nib[..., 0::2] = words & 0xF
        nib[..., 1::2] = words >> 4
        vals = E2M1[nib]
    vals = vals * np.repeat(np.exp2(scales.astype(np.float64) - 127.0), 8, axis=1)[..., None]
    return vals.transpose(0, 1, 3, 2).reshape(g * 512, n)


def sigm(f):
    return 1.0 / (1.0 + np.exp(-np.maximum(f, -700.0)))


K, N, T = 512, 1024, 512


def setup_inputs():
    n = np.random.standard_normal
    s = mx_kscale(K)[:, None]
    p_wg = pack_weight(n((K, N)) / np.sqrt(K) / s, "e2m1")
    p_wh = pack_weight(n((K, N)) / np.sqrt(K) / s, "e2m1")
    return {
        "x": (n((K, T)) * s).astype(np.float32),
        "wg_words": p_wg[0],
        "wg_scales": p_wg[1],
        "wh_words": p_wh[0],
        "wh_scales": p_wh[1],
        "bg": (0.3 * n(N) - 1.0).astype(np.float32),
        "res": (n((N, T))).astype(np.float32),
    }


def reference(x, wg_words, wg_scales, wh_words, wh_scales, bg, res):
    x_ = mxq(f64(x), 0, "e4m3")
    wg_ = unpack_weight(wg_words, wg_scales, "e2m1")
    wh_ = unpack_weight(wh_words, wh_scales, "e2m1")
    ga = wg_.T @ x_
    gate = sigm(ga + f64(bg)[:, None])
    ha = wh_.T @ x_
    return f64(res) + gate * (np.maximum(ha, 0.0) - f64(res))

@@ -1,0 +1,271 @@
+from contextlib import ExitStack
+
+import concourse.mybir as mybir
+from concourse.masks import make_identity
+
+K, N, T = 512, 1024, 512
+FLOPS = 2 * 2 * K * N * T
+
+F32 = mybir.dt.float32
+BF16 = mybir.dt.bfloat16
+I32 = mybir.dt.int32
+U32 = mybir.dt.uint32
+U8 = mybir.dt.uint8
+FP8X4 = mybir.dt.float8_e4m3fn_x4
+FP4X4 = mybir.dt.float4_e2m1fn_x4
+ALU = mybir.AluOpType
+ACT = mybir.ActivationFunctionType
+
+P = 128
+HALF = T // 2
+BANK = 512
+MODES = "A"
+CHUNKS = [(j, 1, 0, T) for j in range(8)]
+
+
+def tile_mix_hway_relu_none_kernel(tc, x, wg_words, wg_scales, wh_words, wh_scales, bg, res, out):
+    nc = tc.nc
+    with ExitStack() as ctx:
+        sb = ctx.enter_context(tc.tile_pool(name="sb", bufs=1))
+        ps = ctx.enter_context(tc.psum_pool(name="ps", bufs=1))
+        ctx.enter_context(tc.manual_schedule())
+
+        def rows_of(dram, c):
+            j0, nj, t0, tw = CHUNKS[c]
+            return dram[j0 * P : (j0 + nj) * P, t0 : t0 + tw].rearrange("(j p) t -> p j t", p=P)
+
+        def as_rows(tile, c):
+            return tile[:].rearrange("p (j t) -> p j t", j=CHUNKS[c][1])
+
+        x_raw = [sb.tile([P, 4, HALF], F32, name=f"x_raw{u}") for u in range(2)]
+        x_bf = [sb.tile([P, HALF, 4], BF16, name=f"x_bf{u}", align_bytes=64) for u in range(2)]
+        x_codes = sb.tile([P, T], U32, align_bytes=64)
+        x_plane = sb.tile([P, T], U8, align_bytes=64)
+        words = {(w, u): sb.tile([P, N], U8, name=f"words_{w}{u}", align_bytes=64) for w in "hg" for u in range(2)}
+        plane = {w: sb.tile([P, N], U8, name=f"plane_{w}", align_bytes=64) for w in "hg"}
+        dram_words = {"h": wh_words, "g": wg_words}
+        dram_scales = {"h": wh_scales, "g": wg_scales}
+        bias_rows = sb.tile([P, P], F32)
+        bias = sb.tile([P, 8], F32)
+        ident = sb.tile([P, P], F32)
+        warm = sb.tile([P, 2], F32)
+        res_sb = [sb.tile([P, BANK], F32, name=f"res{c}") for c in range(8)]
+        gate = [sb.tile([P, BANK], F32, name=f"gate{c}") for c in range(8)]
+        diff = [sb.tile([P, BANK], F32, name=f"diff{c}") for c in range(8)]
+        prod = [sb.tile([P, BANK], F32, name=f"prod{c}") for c in range(8)]
+        out_t = [sb.tile([P, BANK], F32, name=f"out_t{c}") for c in range(8)]
+        out_sb = [sb.tile([P, BANK], F32, name=f"out{c}") for c in range(8)]
+        acc = {}
+        held = {}
+        free_banks = list(range(8))
+
+        def take_bank(key):
+            held[key] = free_banks.pop(0)
+            acc[key] = ps.tile([P, BANK], F32, name=f"acc_{key[0]}{key[1]}", tag=f"bank{held[key]}")
+            return acc[key]
+
+        def give_bank(key):
+            free_banks.append(held[key])
+
+        def load_x(u):
+            nc.sync.dma_start(out=x_raw[u][:], in_=x[:, u * HALF : (u + 1) * HALF].rearrange("(p j) t -> p j t", j=4))
+
+        def load_words(w, u):
+            nc.sync.dma_start(out=words[w, u][:].bitcast(I32), in_=dram_words[w][0, :, u * N : (u + 1) * N].bitcast(I32))
+
+        def load_scales(w):
+            rows = dram_scales[w][0].rearrange("(q r) n -> r q n", r=4)
+            for r in range(4):
+                nc.sync.dma_start(out=plane[w][r:P:32, :].bitcast(I32), in_=rows[r].bitcast(I32))
+
+        def load_res(c):
+            nc.sync.dma_start(out=as_rows(res_sb[c], c), in_=rows_of(res, c))
+
+        def interleave(copy, u, c0, c1):
+            copy(
+                out=x_bf[u][:, c0:c1, :].rearrange("p (c i) j -> p c j i", i=4),
+                in_=x_raw[u][:, :, c0:c1].rearrange("p j (c i) -> p c j i", i=4),
+            )
+
+        def quantize(u, c0, c1):
+            cols = slice(u * HALF + c0, u * HALF + c1)
+            nc.vector.quantize_mx(
+                out=x_codes[:, cols].bitcast(FP8X4),
+                scales=x_plane[:, cols],
+                in_=x_bf[u][:, c0:c1, :].rearrange("p c j -> p (c j)"),
+            )
+
+        def multiply(w, j, t0=0, t1=T):
+            if t0 == 0:
+                take_bank((w, j))
+            nc.tensor.matmul_mx(
+                out=acc[w, j][:, t0:t1],
+                lhsT=words[w, j // 4][:, 2 * P * (j % 4) : 2 * P * (j % 4 + 1)].bitcast(FP4X4),
+                lhsT_scale=plane[w][:, P * j : P * (j + 1)],
+                rhs=x_codes[:, t0:t1].bitcast(FP8X4),
+                rhs_scale=x_plane[:, t0:t1],
+                start=True,
+                stop=True,
+            )
+
+        def sigmoid(c):
+            j0, nj, t0, tw = CHUNKS[c]
+            for i in range(nj):
+                cols = slice(i * tw, (i + 1) * tw)
+                nc.scalar.activation(
+                    out=gate[c][:, cols], in_=acc["g", c][:, cols], func=ACT.Sigmoid, bias=bias[:, j0 + i : j0 + i + 1]
+                )
+            give_bank(("g", c))
+
+        def subtract(c):
+            nc.vector.scalar_tensor_tensor(
+                out=diff[c][:], in0=acc["h", c][:], scalar=0.0, in1=res_sb[c][:], op0=ALU.max, op1=ALU.subtract
+            )
+            give_bank(("h", c))
+
+        def scale(c):
+            nc.vector.tensor_tensor(out=prod[c][:], in0=diff[c][:], in1=gate[c][:], op=ALU.mult)
+
+        def store(c):
+            nc.sync.dma_start(out=rows_of(out, c), in_=as_rows(out_sb[c], c))
+
+        def add_on_vector(c):
+            nc.vector.tensor_tensor(out=out_sb[c][:], in0=prod[c][:], in1=res_sb[c][:], op=ALU.add)
+            store(c)
+
+        def add_on_gpsimd(c):
+            nc.gpsimd.tensor_tensor(out=out_sb[c][:], in0=prod[c][:], in1=res_sb[c][:], op=ALU.add)
+            store(c)
+
+        def turn(dst, src, start, stop):
+            for b in range(4):
+                blk = slice(b * P, (b + 1) * P)
+                nc.tensor.matmul(
+                    out=dst[:, blk], lhsT=src[:, blk], rhs=ident[:], is_transpose=True,
+                    start=start and b == 0, stop=stop and b == 3,
+                )
+
+        def scale_on_gpsimd(c):
+            nc.gpsimd.tensor_tensor(out=prod[c][:], in0=diff[c][:], in1=gate[c][:], op=ALU.mult)
+
+        def turn_res(c):
+            turn(take_bank(("s", c)), res_sb[c], True, False)
+
+        def turn_prod(c):
+            turn(acc["s", c], prod[c], False, True)
+
+        def copy_sum(c):
+            nc.scalar.copy(out=out_t[c][:], in_=acc["s", c][:])
+            give_bank(("s", c))
+
+        def turn_back(c):
+            turn(take_bank(("b", c)), out_t[c], True, True)
+
+        def copy_out(c):
+            nc.scalar.copy(out=out_sb[c][:], in_=acc["b", c][:])
+            give_bank(("b", c))
+            store(c)
+
+        nc.vector.memset(plane["h"][:].bitcast(I32), 0)
+        nc.vector.memset(plane["g"][:].bitcast(I32), 0)
+        nc.vector.memset(bias_rows[:], 0.0)
+        nc.vector.memset(warm[:], 0.0)
+        make_identity(nc, ident[:])
+        load_x(0)
+        load_scales("h")
+        load_words("h", 0)
+        load_x(1)
+        load_res(0)
+        nc.sync.dma_start(out=bias_rows[0:8, :], in_=bg.rearrange("(j p) -> j p", p=P))
+        load_words("g", 0)
+        load_scales("g")
+        load_res(1)
+        load_res(2)
+        load_res(3)
+        load_words("h", 1)
+        load_words("g", 1)
+        load_res(4)
+        load_res(5)
+        load_res(6)
+        load_res(7)
+        nc.scalar.activation(out=warm[:, 1:2], in_=warm[:, 0:1], func=ACT.Sigmoid)
+
+        interleave(nc.vector.tensor_copy, 0, 0, P)
+        interleave(nc.vector.tensor_copy, 0, P, HALF)
+        quantize(0, 0, P)
+        quantize(0, P, HALF)
+        for j in range(4):
+            multiply("h", j, 0, HALF)
+        interleave(nc.vector.tensor_copy, 1, 0, P)
+        interleave(nc.vector.tensor_copy, 1, P, 176)
+        interleave(nc.scalar.copy, 1, 176, HALF)
+        quantize(1, 0, P)
+        quantize(1, P, HALF)
+        bias_t = take_bank(("bias", 0))
+        nc.tensor.transpose(bias_t[:, 0:P], bias_rows[:], ident[:])
+        nc.scalar.copy(out=bias[:], in_=bias_t[:, 0:8])
+        give_bank(("bias", 0))
+        multiply("h", 0, HALF, T)
+        multiply("g", 0)
+        sigmoid(0)
+        subtract(0)
+        multiply("h", 1, HALF, T)
+        multiply("g", 1)
+        sigmoid(1)
+        subtract(1)
+        multiply("h", 2, HALF, T)
+        multiply("g", 2)
+        sigmoid(2)
+        scale(0)
+        subtract(2)
+        multiply("h", 3, HALF, T)
+        multiply("g", 3)
+        sigmoid(3)
+        scale(1)
+        subtract(3)
+        turn_res(0)
+        turn_prod(0)
+        copy_sum(0)
+        scale(2)
+        multiply("h", 4)
+        multiply("g", 4)
+        sigmoid(4)
+        subtract(4)
+        turn_res(1)
+        turn_prod(1)
+        turn_back(0)
+        copy_sum(1)
+        copy_out(0)
+        scale(3)
+        multiply("h", 5)
+        multiply("g", 5)
+        sigmoid(5)
+        subtract(5)
+        turn_res(2)
+        turn_prod(2)
+        turn_back(1)
+        copy_sum(2)
+        copy_out(1)
+        scale(4)
+        multiply("h", 6)
+        multiply("g", 6)
+        sigmoid(6)
+        subtract(6)
+        add_on_vector(4)
+        turn_res(3)
+        turn_prod(3)
+        turn_back(2)
+        copy_sum(3)
+        copy_out(2)
+        scale(5)
+        multiply("h", 7)
+        multiply("g", 7)
+        sigmoid(7)
+        subtract(7)
+        add_on_vector(5)
+        turn_back(3)
+        copy_out(3)
+        scale(6)
+        scale(7)
+        add_on_vector(6)
+        add_on_vector(7)

@@ -131,7 +131,6 @@ def tile_mix_hway_relu_none_kernel(tc, x, wg_words, wg_scales, wh_words, wh_scal
 
         def add_on_vector(c):
             nc.vector.tensor_tensor(out=out_sb[c][:], in0=prod[c][:], in1=res_sb[c][:], op=ALU.add)
-            store(c)
 
         def add_on_gpsimd(c):
             nc.gpsimd.tensor_tensor(out=out_sb[c][:], in0=prod[c][:], in1=res_sb[c][:], op=ALU.add)
@@ -164,7 +163,6 @@ def tile_mix_hway_relu_none_kernel(tc, x, wg_words, wg_scales, wh_words, wh_scal
         def copy_out(c):
             nc.scalar.copy(out=out_sb[c][:], in_=acc["b", c][:])
             give_bank(("b", c))
-            store(c)
 
         nc.vector.memset(plane["h"][:].bitcast(I32), 0)
         nc.vector.memset(plane["g"][:].bitcast(I32), 0)
@@ -180,10 +178,10 @@ def tile_mix_hway_relu_none_kernel(tc, x, wg_words, wg_scales, wh_words, wh_scal
         load_words("g", 0)
         load_scales("g")
         load_res(1)
-        load_res(2)
-        load_res(3)
         load_words("h", 1)
+        load_res(2)
         load_words("g", 1)
+        load_res(3)
         load_res(4)
         load_res(5)
         load_res(6)
@@ -216,56 +214,58 @@ def tile_mix_hway_relu_none_kernel(tc, x, wg_words, wg_scales, wh_words, wh_scal
         multiply("h", 2, HALF, T)
         multiply("g", 2)
         sigmoid(2)
-        scale(0)
-        subtract(2)
         multiply("h", 3, HALF, T)
         multiply("g", 3)
         sigmoid(3)
+        scale(0)
         scale(1)
+        subtract(2)
         subtract(3)
+        scale_on_gpsimd(2)
+        scale_on_gpsimd(3)
+        multiply("h", 4)
+        multiply("h", 5)
+        multiply("h", 6)
+        multiply("h", 7)
+        subtract(4)
+        subtract(5)
+        subtract(6)
+        subtract(7)
+        multiply("g", 4)
+        multiply("g", 5)
+        sigmoid(4)
+        sigmoid(5)
         turn_res(0)
         turn_prod(0)
-        copy_sum(0)
-        scale(2)
-        multiply("h", 4)
-        multiply("g", 4)
-        sigmoid(4)
-        subtract(4)
         turn_res(1)
         turn_prod(1)
-        turn_back(0)
+        copy_sum(0)
         copy_sum(1)
-        copy_out(0)
-        scale(3)
-        multiply("h", 5)
-        multiply("g", 5)
-        sigmoid(5)
-        subtract(5)
-        turn_res(2)
-        turn_prod(2)
-        turn_back(1)
-        copy_sum(2)
-        copy_out(1)
-        scale(4)
-        multiply("h", 6)
         multiply("g", 6)
-        sigmoid(6)
-        subtract(6)
-        add_on_vector(4)
-        turn_res(3)
-        turn_prod(3)
-        turn_back(2)
-        copy_sum(3)
-        copy_out(2)
-        scale(5)
-        multiply("h", 7)
         multiply("g", 7)
+        turn_back(0)
+        turn_back(1)
+        sigmoid(6)
+        copy_out(0)
+        copy_out(1)
         sigmoid(7)
-        subtract(7)
-        add_on_vector(5)
-        turn_back(3)
-        copy_out(3)
+        add_on_vector(2)
+        store(2)
+        store(0)
+        scale(4)
+        add_on_vector(3)
+        store(1)
+        store(3)
+        scale(5)
+        add_on_vector(4)
+        store(4)
         scale(6)
-        scale(7)
+        add_on_vector(5)
+        store(5)
         add_on_vector(6)
-        add_on_vector(7)
+        store(6)
+        for cols in (slice(0, HALF), slice(HALF, T)):
+            nc.vector.tensor_tensor(out=prod[7][:, cols], in0=diff[7][:, cols], in1=gate[7][:, cols], op=ALU.mult)
+        for cols in (slice(0, HALF), slice(HALF, T)):
+            nc.vector.tensor_tensor(out=out_sb[7][:, cols], in0=prod[7][:, cols], in1=res_sb[7][:, cols], op=ALU.add)
+            nc.sync.dma_start(out=out[7 * P : 8 * P, cols], in_=out_sb[7][:, cols])

@@ -17,10 +17,18 @@ ALU = mybir.AluOpType
 ACT = mybir.ActivationFunctionType
 
 P = 128
+PACK = 4
+WORD_BYTES = 2
+QUADRANT = 32
+TILES = N // P
+EARLY_TILES = TILES // 2
 HALF = T // 2
-BANK = 512
-MODES = "A"
-CHUNKS = [(j, 1, 0, T) for j in range(8)]
+BANKS = 8
+
+VECTOR_COLUMNS = 176
+
+TENSOR_ADD_TILES = (0, 1)
+GPSIMD_PROD_TILES = (2, 3)
 
 
 def tile_mix_hway_relu_none_kernel(tc, x, wg_words, wg_scales, wh_words, wh_scales, bg, res, out):
@@ -30,61 +38,66 @@ def tile_mix_hway_relu_none_kernel(tc, x, wg_words, wg_scales, wh_words, wh_scal
         ps = ctx.enter_context(tc.psum_pool(name="ps", bufs=1))
         ctx.enter_context(tc.manual_schedule())
 
-        def rows_of(dram, c):
-            j0, nj, t0, tw = CHUNKS[c]
-            return dram[j0 * P : (j0 + nj) * P, t0 : t0 + tw].rearrange("(j p) t -> p j t", p=P)
-
-        def as_rows(tile, c):
-            return tile[:].rearrange("p (j t) -> p j t", j=CHUNKS[c][1])
-
-        x_raw = [sb.tile([P, 4, HALF], F32, name=f"x_raw{u}") for u in range(2)]
-        x_bf = [sb.tile([P, HALF, 4], BF16, name=f"x_bf{u}", align_bytes=64) for u in range(2)]
+        x_raw = [sb.tile([P, PACK, HALF], F32, name=f"x_raw{u}") for u in range(2)]
+        x_bf = [sb.tile([P, HALF, PACK], BF16, name=f"x_bf{u}", align_bytes=64) for u in range(2)]
         x_codes = sb.tile([P, T], U32, align_bytes=64)
         x_plane = sb.tile([P, T], U8, align_bytes=64)
-        words = {(w, u): sb.tile([P, N], U8, name=f"words_{w}{u}", align_bytes=64) for w in "hg" for u in range(2)}
+        half_bytes = WORD_BYTES * EARLY_TILES * P
+        words = {
+            (w, u): sb.tile([P, half_bytes], U8, name=f"words_{w}{u}", align_bytes=64) for w in "hg" for u in range(2)
+        }
         plane = {w: sb.tile([P, N], U8, name=f"plane_{w}", align_bytes=64) for w in "hg"}
         dram_words = {"h": wh_words, "g": wg_words}
         dram_scales = {"h": wh_scales, "g": wg_scales}
         bias_rows = sb.tile([P, P], F32)
-        bias = sb.tile([P, 8], F32)
+        bias = sb.tile([P, TILES], F32)
         ident = sb.tile([P, P], F32)
         warm = sb.tile([P, 2], F32)
-        res_sb = [sb.tile([P, BANK], F32, name=f"res{c}") for c in range(8)]
-        gate = [sb.tile([P, BANK], F32, name=f"gate{c}") for c in range(8)]
-        diff = [sb.tile([P, BANK], F32, name=f"diff{c}") for c in range(8)]
-        prod = [sb.tile([P, BANK], F32, name=f"prod{c}") for c in range(8)]
-        out_t = [sb.tile([P, BANK], F32, name=f"out_t{c}") for c in range(8)]
-        out_sb = [sb.tile([P, BANK], F32, name=f"out{c}") for c in range(8)]
-        acc = {}
-        held = {}
-        free_banks = list(range(8))
+        res_sb = [sb.tile([P, T], F32, name=f"res{j}") for j in range(TILES)]
+        gate = [sb.tile([P, T], F32, name=f"gate{j}") for j in range(TILES)]
+        diff = [sb.tile([P, T], F32, name=f"diff{j}") for j in range(TILES)]
+        prod = [sb.tile([P, T], F32, name=f"prod{j}") for j in range(TILES)]
+        out_turned = {j: sb.tile([P, T], F32, name=f"out_turned{j}") for j in TENSOR_ADD_TILES}
+        out_sb = [sb.tile([P, T], F32, name=f"out{j}") for j in range(TILES)]
 
-        def take_bank(key):
-            held[key] = free_banks.pop(0)
-            acc[key] = ps.tile([P, BANK], F32, name=f"acc_{key[0]}{key[1]}", tag=f"bank{held[key]}")
-            return acc[key]
+        bank_tile = {}
+        bank_number = {}
+        free_banks = list(range(BANKS))
 
-        def give_bank(key):
-            free_banks.append(held[key])
+        def take_bank(role, j):
+            bank_number[role, j] = free_banks.pop(0)
+            bank_tile[role, j] = ps.tile([P, T], F32, name=f"bank_{role}{j}", tag=f"bank{bank_number[role, j]}")
+            return bank_tile[role, j]
+
+        def give_bank(role, j):
+            free_banks.append(bank_number[role, j])
+
+        def rows(j):
+            return slice(j * P, (j + 1) * P)
 
         def load_x(u):
-            nc.sync.dma_start(out=x_raw[u][:], in_=x[:, u * HALF : (u + 1) * HALF].rearrange("(p j) t -> p j t", j=4))
+            source = x[:, u * HALF : (u + 1) * HALF].rearrange("(p i) t -> p i t", i=PACK)
+            nc.sync.dma_start(out=x_raw[u][:], in_=source)
 
         def load_words(w, u):
-            nc.sync.dma_start(out=words[w, u][:].bitcast(I32), in_=dram_words[w][0, :, u * N : (u + 1) * N].bitcast(I32))
+            source = dram_words[w][0, :, u * half_bytes : (u + 1) * half_bytes]
+            nc.sync.dma_start(out=words[w, u][:].bitcast(I32), in_=source.bitcast(I32))
 
         def load_scales(w):
-            rows = dram_scales[w][0].rearrange("(q r) n -> r q n", r=4)
-            for r in range(4):
-                nc.sync.dma_start(out=plane[w][r:P:32, :].bitcast(I32), in_=rows[r].bitcast(I32))
+            by_r = dram_scales[w][0].rearrange("(q r) n -> r q n", r=PACK)
+            for r in range(PACK):
+                nc.sync.dma_start(out=plane[w][r:P:QUADRANT, :].bitcast(I32), in_=by_r[r].bitcast(I32))
 
-        def load_res(c):
-            nc.sync.dma_start(out=as_rows(res_sb[c], c), in_=rows_of(res, c))
+        def load_res(j):
+            nc.sync.dma_start(out=res_sb[j][:], in_=res[rows(j), :])
+
+        def store(j, cols=slice(0, T)):
+            nc.sync.dma_start(out=out[rows(j), cols], in_=out_sb[j][:, cols])
 
         def interleave(copy, u, c0, c1):
             copy(
-                out=x_bf[u][:, c0:c1, :].rearrange("p (c i) j -> p c j i", i=4),
-                in_=x_raw[u][:, :, c0:c1].rearrange("p j (c i) -> p c j i", i=4),
+                out=x_bf[u][:, c0:c1, :].rearrange("p (c e) i -> p c i e", e=4),
+                in_=x_raw[u][:, :, c0:c1].rearrange("p i (c e) -> p c i e", e=4),
             )
 
         def quantize(u, c0, c1):
@@ -92,180 +105,152 @@ def tile_mix_hway_relu_none_kernel(tc, x, wg_words, wg_scales, wh_words, wh_scal
             nc.vector.quantize_mx(
                 out=x_codes[:, cols].bitcast(FP8X4),
                 scales=x_plane[:, cols],
-                in_=x_bf[u][:, c0:c1, :].rearrange("p c j -> p (c j)"),
+                in_=x_bf[u][:, c0:c1, :].rearrange("p c i -> p (c i)"),
             )
 
         def multiply(w, j, t0=0, t1=T):
             if t0 == 0:
-                take_bank((w, j))
+                take_bank(w, j)
+            u, place = divmod(j, EARLY_TILES)
             nc.tensor.matmul_mx(
-                out=acc[w, j][:, t0:t1],
-                lhsT=words[w, j // 4][:, 2 * P * (j % 4) : 2 * P * (j % 4 + 1)].bitcast(FP4X4),
-                lhsT_scale=plane[w][:, P * j : P * (j + 1)],
+                out=bank_tile[w, j][:, t0:t1],
+                lhsT=words[w, u][:, WORD_BYTES * P * place : WORD_BYTES * P * (place + 1)].bitcast(FP4X4),
+                lhsT_scale=plane[w][:, rows(j)],
                 rhs=x_codes[:, t0:t1].bitcast(FP8X4),
                 rhs_scale=x_plane[:, t0:t1],
                 start=True,
                 stop=True,
             )
 
-        def sigmoid(c):
-            j0, nj, t0, tw = CHUNKS[c]
-            for i in range(nj):
-                cols = slice(i * tw, (i + 1) * tw)
-                nc.scalar.activation(
-                    out=gate[c][:, cols], in_=acc["g", c][:, cols], func=ACT.Sigmoid, bias=bias[:, j0 + i : j0 + i + 1]
-                )
-            give_bank(("g", c))
+        def make_gate(j):
+            nc.scalar.activation(out=gate[j][:], in_=bank_tile["g", j][:], func=ACT.Sigmoid, bias=bias[:, j : j + 1])
+            give_bank("g", j)
 
-        def subtract(c):
+        def make_diff(j):
             nc.vector.scalar_tensor_tensor(
-                out=diff[c][:], in0=acc["h", c][:], scalar=0.0, in1=res_sb[c][:], op0=ALU.max, op1=ALU.subtract
+                out=diff[j][:], in0=bank_tile["h", j][:], scalar=0.0, in1=res_sb[j][:], op0=ALU.max, op1=ALU.subtract
             )
-            give_bank(("h", c))
+            give_bank("h", j)
 
-        def scale(c):
-            nc.vector.tensor_tensor(out=prod[c][:], in0=diff[c][:], in1=gate[c][:], op=ALU.mult)
+        def make_prod(engine, j, cols=slice(0, T)):
+            engine.tensor_tensor(out=prod[j][:, cols], in0=diff[j][:, cols], in1=gate[j][:, cols], op=ALU.mult)
 
-        def store(c):
-            nc.sync.dma_start(out=rows_of(out, c), in_=as_rows(out_sb[c], c))
+        def add_on_vector(j, cols=slice(0, T)):
+            nc.vector.tensor_tensor(out=out_sb[j][:, cols], in0=prod[j][:, cols], in1=res_sb[j][:, cols], op=ALU.add)
 
-        def add_on_vector(c):
-            nc.vector.tensor_tensor(out=out_sb[c][:], in0=prod[c][:], in1=res_sb[c][:], op=ALU.add)
-
-        def add_on_gpsimd(c):
-            nc.gpsimd.tensor_tensor(out=out_sb[c][:], in0=prod[c][:], in1=res_sb[c][:], op=ALU.add)
-            store(c)
-
-        def turn(dst, src, start, stop):
-            for b in range(4):
-                blk = slice(b * P, (b + 1) * P)
+        def turn(bank, source, start, stop):
+            blocks = T // P
+            for b in range(blocks):
                 nc.tensor.matmul(
-                    out=dst[:, blk], lhsT=src[:, blk], rhs=ident[:], is_transpose=True,
-                    start=start and b == 0, stop=stop and b == 3,
+                    out=bank[:, b * P : (b + 1) * P],
+                    lhsT=source[:, b * P : (b + 1) * P],
+                    rhs=ident[:],
+                    is_transpose=True,
+                    start=start and b == 0,
+                    stop=stop and b == blocks - 1,
                 )
 
-        def scale_on_gpsimd(c):
-            nc.gpsimd.tensor_tensor(out=prod[c][:], in0=diff[c][:], in1=gate[c][:], op=ALU.mult)
+        def add_turned(j):
+            bank = take_bank("sum", j)
+            turn(bank, res_sb[j], True, False)
+            turn(bank, prod[j], False, True)
 
-        def turn_res(c):
-            turn(take_bank(("s", c)), res_sb[c], True, False)
-
-        def turn_prod(c):
-            turn(acc["s", c], prod[c], False, True)
-
-        def copy_sum(c):
-            nc.scalar.copy(out=out_t[c][:], in_=acc["s", c][:])
-            give_bank(("s", c))
-
-        def turn_back(c):
-            turn(take_bank(("b", c)), out_t[c], True, True)
-
-        def copy_out(c):
-            nc.scalar.copy(out=out_sb[c][:], in_=acc["b", c][:])
-            give_bank(("b", c))
+        def copy_out_of(role, j, target):
+            nc.scalar.copy(out=target[:], in_=bank_tile[role, j][:])
+            give_bank(role, j)
 
         nc.vector.memset(plane["h"][:].bitcast(I32), 0)
         nc.vector.memset(plane["g"][:].bitcast(I32), 0)
         nc.vector.memset(bias_rows[:], 0.0)
         nc.vector.memset(warm[:], 0.0)
         make_identity(nc, ident[:])
+
         load_x(0)
         load_scales("h")
+        nc.sync.dma_start(out=bias_rows[0:TILES, :], in_=bg.rearrange("(j p) -> j p", p=P))
         load_words("h", 0)
         load_x(1)
         load_res(0)
-        nc.sync.dma_start(out=bias_rows[0:8, :], in_=bg.rearrange("(j p) -> j p", p=P))
         load_words("g", 0)
         load_scales("g")
         load_res(1)
-        load_words("h", 1)
         load_res(2)
-        load_words("g", 1)
+        load_words("h", 1)
         load_res(3)
-        load_res(4)
-        load_res(5)
-        load_res(6)
-        load_res(7)
+        load_words("g", 1)
+        for j in range(EARLY_TILES, TILES):
+            load_res(j)
+
         nc.scalar.activation(out=warm[:, 1:2], in_=warm[:, 0:1], func=ACT.Sigmoid)
+
+        bias_bank = take_bank("bias", 0)
+        nc.tensor.transpose(bias_bank[:, 0:P], bias_rows[:], ident[:])
+        nc.scalar.copy(out=bias[:], in_=bias_bank[:, 0:TILES])
+        give_bank("bias", 0)
 
         interleave(nc.vector.tensor_copy, 0, 0, P)
         interleave(nc.vector.tensor_copy, 0, P, HALF)
         quantize(0, 0, P)
         quantize(0, P, HALF)
-        for j in range(4):
+        for j in range(EARLY_TILES):
             multiply("h", j, 0, HALF)
         interleave(nc.vector.tensor_copy, 1, 0, P)
-        interleave(nc.vector.tensor_copy, 1, P, 176)
-        interleave(nc.scalar.copy, 1, 176, HALF)
+        interleave(nc.vector.tensor_copy, 1, P, VECTOR_COLUMNS)
+        interleave(nc.scalar.copy, 1, VECTOR_COLUMNS, HALF)
         quantize(1, 0, P)
         quantize(1, P, HALF)
-        bias_t = take_bank(("bias", 0))
-        nc.tensor.transpose(bias_t[:, 0:P], bias_rows[:], ident[:])
-        nc.scalar.copy(out=bias[:], in_=bias_t[:, 0:8])
-        give_bank(("bias", 0))
-        multiply("h", 0, HALF, T)
-        multiply("g", 0)
-        sigmoid(0)
-        subtract(0)
-        multiply("h", 1, HALF, T)
-        multiply("g", 1)
-        sigmoid(1)
-        subtract(1)
-        multiply("h", 2, HALF, T)
-        multiply("g", 2)
-        sigmoid(2)
-        multiply("h", 3, HALF, T)
-        multiply("g", 3)
-        sigmoid(3)
-        scale(0)
-        scale(1)
-        subtract(2)
-        subtract(3)
-        scale_on_gpsimd(2)
-        scale_on_gpsimd(3)
-        multiply("h", 4)
-        multiply("h", 5)
-        multiply("h", 6)
-        multiply("h", 7)
-        subtract(4)
-        subtract(5)
-        subtract(6)
-        subtract(7)
-        multiply("g", 4)
-        multiply("g", 5)
-        sigmoid(4)
-        sigmoid(5)
-        turn_res(0)
-        turn_prod(0)
-        turn_res(1)
-        turn_prod(1)
-        copy_sum(0)
-        copy_sum(1)
-        multiply("g", 6)
-        multiply("g", 7)
-        turn_back(0)
-        turn_back(1)
-        sigmoid(6)
-        copy_out(0)
-        copy_out(1)
-        sigmoid(7)
-        add_on_vector(2)
-        store(2)
-        store(0)
-        scale(4)
-        add_on_vector(3)
-        store(1)
-        store(3)
-        scale(5)
-        add_on_vector(4)
-        store(4)
-        scale(6)
-        add_on_vector(5)
-        store(5)
-        add_on_vector(6)
-        store(6)
-        for cols in (slice(0, HALF), slice(HALF, T)):
-            nc.vector.tensor_tensor(out=prod[7][:, cols], in0=diff[7][:, cols], in1=gate[7][:, cols], op=ALU.mult)
-        for cols in (slice(0, HALF), slice(HALF, T)):
-            nc.vector.tensor_tensor(out=out_sb[7][:, cols], in0=prod[7][:, cols], in1=res_sb[7][:, cols], op=ALU.add)
-            nc.sync.dma_start(out=out[7 * P : 8 * P, cols], in_=out_sb[7][:, cols])
+
+        for j in range(EARLY_TILES):
+            multiply("h", j, HALF, T)
+            multiply("g", j)
+            make_gate(j)
+            if j in TENSOR_ADD_TILES:
+                make_diff(j)
+        for j in TENSOR_ADD_TILES:
+            make_prod(nc.vector, j)
+
+        for j in GPSIMD_PROD_TILES:
+            make_diff(j)
+        for j in GPSIMD_PROD_TILES:
+            make_prod(nc.gpsimd, j)
+        late_tiles = range(EARLY_TILES, TILES)
+        for j in late_tiles:
+            multiply("h", j)
+        for j in late_tiles:
+            make_diff(j)
+
+        first_pair, second_pair = late_tiles[:2], late_tiles[2:]
+        for j in first_pair:
+            multiply("g", j)
+        for j in first_pair:
+            make_gate(j)
+        for j in TENSOR_ADD_TILES:
+            add_turned(j)
+        for j in TENSOR_ADD_TILES:
+            copy_out_of("sum", j, out_turned[j])
+        for j in second_pair:
+            multiply("g", j)
+        for j in TENSOR_ADD_TILES:
+            turn(take_bank("back", j), out_turned[j], True, True)
+        make_gate(second_pair[0])
+        for j in TENSOR_ADD_TILES:
+            copy_out_of("back", j, out_sb[j])
+        make_gate(second_pair[1])
+
+        last = TILES - 1
+        add_on_vector(GPSIMD_PROD_TILES[0])
+        store(GPSIMD_PROD_TILES[0])
+        store(TENSOR_ADD_TILES[0])
+        for j in range(GPSIMD_PROD_TILES[1], last):
+            if j + 1 < last:
+                make_prod(nc.vector, j + 1)
+            add_on_vector(j)
+            if j == GPSIMD_PROD_TILES[1]:
+                store(TENSOR_ADD_TILES[1])
+            store(j)
+        halves = (slice(0, HALF), slice(HALF, T))
+        for cols in halves:
+            make_prod(nc.vector, last, cols)
+        for cols in halves:
+            add_on_vector(last, cols)
+            store(last, cols)

from contextlib import ExitStack

import concourse.mybir as mybir
from concourse.masks import make_identity

K, N, T = 512, 1024, 512
FLOPS = 2 * 2 * K * N * T

F32 = mybir.dt.float32
BF16 = mybir.dt.bfloat16
I32 = mybir.dt.int32
U32 = mybir.dt.uint32
U8 = mybir.dt.uint8
FP8X4 = mybir.dt.float8_e4m3fn_x4
FP4X4 = mybir.dt.float4_e2m1fn_x4
ALU = mybir.AluOpType
ACT = mybir.ActivationFunctionType

P = 128
PACK = 4
WORD_BYTES = 2
QUADRANT = 32
TILES = N // P
EARLY_TILES = TILES // 2
HALF = T // 2
BANKS = 8

VECTOR_COLUMNS = 176

TENSOR_ADD_TILES = (0, 1)
GPSIMD_PROD_TILES = (2, 3)


def tile_mix_hway_relu_none_kernel(tc, x, wg_words, wg_scales, wh_words, wh_scales, bg, res, out):
    nc = tc.nc
    with ExitStack() as ctx:
        sb = ctx.enter_context(tc.tile_pool(name="sb", bufs=1))
        ps = ctx.enter_context(tc.psum_pool(name="ps", bufs=1))
        ctx.enter_context(tc.manual_schedule())

        x_raw = [sb.tile([P, PACK, HALF], F32, name=f"x_raw{u}") for u in range(2)]
        x_bf = [sb.tile([P, HALF, PACK], BF16, name=f"x_bf{u}", align_bytes=64) for u in range(2)]
        x_codes = sb.tile([P, T], U32, align_bytes=64)
        x_plane = sb.tile([P, T], U8, align_bytes=64)
        half_bytes = WORD_BYTES * EARLY_TILES * P
        words = {
            (w, u): sb.tile([P, half_bytes], U8, name=f"words_{w}{u}", align_bytes=64) for w in "hg" for u in range(2)
        }
        plane = {w: sb.tile([P, N], U8, name=f"plane_{w}", align_bytes=64) for w in "hg"}
        dram_words = {"h": wh_words, "g": wg_words}
        dram_scales = {"h": wh_scales, "g": wg_scales}
        bias_rows = sb.tile([P, P], F32)
        bias = sb.tile([P, TILES], F32)
        ident = sb.tile([P, P], F32)
        warm = sb.tile([P, 2], F32)
        res_sb = [sb.tile([P, T], F32, name=f"res{j}") for j in range(TILES)]
        gate = [sb.tile([P, T], F32, name=f"gate{j}") for j in range(TILES)]
        diff = [sb.tile([P, T], F32, name=f"diff{j}") for j in range(TILES)]
        prod = [sb.tile([P, T], F32, name=f"prod{j}") for j in range(TILES)]
        out_turned = {j: sb.tile([P, T], F32, name=f"out_turned{j}") for j in TENSOR_ADD_TILES}
        out_sb = [sb.tile([P, T], F32, name=f"out{j}") for j in range(TILES)]

        bank_tile = {}
        bank_number = {}
        free_banks = list(range(BANKS))

        def take_bank(role, j):
            bank_number[role, j] = free_banks.pop(0)
            bank_tile[role, j] = ps.tile([P, T], F32, name=f"bank_{role}{j}", tag=f"bank{bank_number[role, j]}")
            return bank_tile[role, j]

        def give_bank(role, j):
            free_banks.append(bank_number[role, j])

        def rows(j):
            return slice(j * P, (j + 1) * P)

        def load_x(u):
            source = x[:, u * HALF : (u + 1) * HALF].rearrange("(p i) t -> p i t", i=PACK)
            nc.sync.dma_start(out=x_raw[u][:], in_=source)

        def load_words(w, u):
            source = dram_words[w][0, :, u * half_bytes : (u + 1) * half_bytes]
            nc.sync.dma_start(out=words[w, u][:].bitcast(I32), in_=source.bitcast(I32))

        def load_scales(w):
            by_r = dram_scales[w][0].rearrange("(q r) n -> r q n", r=PACK)
            for r in range(PACK):
                nc.sync.dma_start(out=plane[w][r:P:QUADRANT, :].bitcast(I32), in_=by_r[r].bitcast(I32))

        def load_res(j):
            nc.sync.dma_start(out=res_sb[j][:], in_=res[rows(j), :])

        def store(j, cols=slice(0, T)):
            nc.sync.dma_start(out=out[rows(j), cols], in_=out_sb[j][:, cols])

        def interleave(copy, u, c0, c1):
            copy(
                out=x_bf[u][:, c0:c1, :].rearrange("p (c e) i -> p c i e", e=4),
                in_=x_raw[u][:, :, c0:c1].rearrange("p i (c e) -> p c i e", e=4),
            )

        def quantize(u, c0, c1):
            cols = slice(u * HALF + c0, u * HALF + c1)
            nc.vector.quantize_mx(
                out=x_codes[:, cols].bitcast(FP8X4),
                scales=x_plane[:, cols],
                in_=x_bf[u][:, c0:c1, :].rearrange("p c i -> p (c i)"),
            )

        def multiply(w, j, t0=0, t1=T):
            if t0 == 0:
                take_bank(w, j)
            u, place = divmod(j, EARLY_TILES)
            nc.tensor.matmul_mx(
                out=bank_tile[w, j][:, t0:t1],
                lhsT=words[w, u][:, WORD_BYTES * P * place : WORD_BYTES * P * (place + 1)].bitcast(FP4X4),
                lhsT_scale=plane[w][:, rows(j)],
                rhs=x_codes[:, t0:t1].bitcast(FP8X4),
                rhs_scale=x_plane[:, t0:t1],
                start=True,
                stop=True,
            )

        def make_gate(j):
            nc.scalar.activation(out=gate[j][:], in_=bank_tile["g", j][:], func=ACT.Sigmoid, bias=bias[:, j : j + 1])
            give_bank("g", j)

        def make_diff(j):
            nc.vector.scalar_tensor_tensor(
                out=diff[j][:], in0=bank_tile["h", j][:], scalar=0.0, in1=res_sb[j][:], op0=ALU.max, op1=ALU.subtract
            )
            give_bank("h", j)

        def make_prod(engine, j, cols=slice(0, T)):
            engine.tensor_tensor(out=prod[j][:, cols], in0=diff[j][:, cols], in1=gate[j][:, cols], op=ALU.mult)

        def add_on_vector(j, cols=slice(0, T)):
            nc.vector.tensor_tensor(out=out_sb[j][:, cols], in0=prod[j][:, cols], in1=res_sb[j][:, cols], op=ALU.add)

        def turn(bank, source, start, stop):
            blocks = T // P
            for b in range(blocks):
                nc.tensor.matmul(
                    out=bank[:, b * P : (b + 1) * P],
                    lhsT=source[:, b * P : (b + 1) * P],
                    rhs=ident[:],
                    is_transpose=True,
                    start=start and b == 0,
                    stop=stop and b == blocks - 1,
                )

        def add_turned(j):
            bank = take_bank("sum", j)
            turn(bank, res_sb[j], True, False)
            turn(bank, prod[j], False, True)

        def copy_out_of(role, j, target):
            nc.scalar.copy(out=target[:], in_=bank_tile[role, j][:])
            give_bank(role, j)

        nc.vector.memset(plane["h"][:].bitcast(I32), 0)
        nc.vector.memset(plane["g"][:].bitcast(I32), 0)
        nc.vector.memset(bias_rows[:], 0.0)
        nc.vector.memset(warm[:], 0.0)
        make_identity(nc, ident[:])

        load_x(0)
        load_scales("h")
        nc.sync.dma_start(out=bias_rows[0:TILES, :], in_=bg.rearrange("(j p) -> j p", p=P))
        load_words("h", 0)
        load_x(1)
        load_res(0)
        load_words("g", 0)
        load_scales("g")
        load_res(1)
        load_res(2)
        load_words("h", 1)
        load_res(3)
        load_words("g", 1)
        for j in range(EARLY_TILES, TILES):
            load_res(j)

        nc.scalar.activation(out=warm[:, 1:2], in_=warm[:, 0:1], func=ACT.Sigmoid)

        bias_bank = take_bank("bias", 0)
        nc.tensor.transpose(bias_bank[:, 0:P], bias_rows[:], ident[:])
        nc.scalar.copy(out=bias[:], in_=bias_bank[:, 0:TILES])
        give_bank("bias", 0)

        interleave(nc.vector.tensor_copy, 0, 0, P)
        interleave(nc.vector.tensor_copy, 0, P, HALF)
        quantize(0, 0, P)
        quantize(0, P, HALF)
        for j in range(EARLY_TILES):
            multiply("h", j, 0, HALF)
        interleave(nc.vector.tensor_copy, 1, 0, P)
        interleave(nc.vector.tensor_copy, 1, P, VECTOR_COLUMNS)
        interleave(nc.scalar.copy, 1, VECTOR_COLUMNS, HALF)
        quantize(1, 0, P)
        quantize(1, P, HALF)

        for j in range(EARLY_TILES):
            multiply("h", j, HALF, T)
            multiply("g", j)
            make_gate(j)
            if j in TENSOR_ADD_TILES:
                make_diff(j)
        for j in TENSOR_ADD_TILES:
            make_prod(nc.vector, j)

        for j in GPSIMD_PROD_TILES:
            make_diff(j)
        for j in GPSIMD_PROD_TILES:
            make_prod(nc.gpsimd, j)
        late_tiles = range(EARLY_TILES, TILES)
        for j in late_tiles:
            multiply("h", j)
        for j in late_tiles:
            make_diff(j)

        first_pair, second_pair = late_tiles[:2], late_tiles[2:]
        for j in first_pair:
            multiply("g", j)
        for j in first_pair:
            make_gate(j)
        for j in TENSOR_ADD_TILES:
            add_turned(j)
        for j in TENSOR_ADD_TILES:
            copy_out_of("sum", j, out_turned[j])
        for j in second_pair:
            multiply("g", j)
        for j in TENSOR_ADD_TILES:
            turn(take_bank("back", j), out_turned[j], True, True)
        make_gate(second_pair[0])
        for j in TENSOR_ADD_TILES:
            copy_out_of("back", j, out_sb[j])
        make_gate(second_pair[1])

        last = TILES - 1
        add_on_vector(GPSIMD_PROD_TILES[0])
        store(GPSIMD_PROD_TILES[0])
        store(TENSOR_ADD_TILES[0])
        for j in range(GPSIMD_PROD_TILES[1], last):
            if j + 1 < last:
                make_prod(nc.vector, j + 1)
            add_on_vector(j)
            if j == GPSIMD_PROD_TILES[1]:
                store(TENSOR_ADD_TILES[1])
            store(j)
        halves = (slice(0, HALF), slice(HALF, T))
        for cols in halves:
            make_prod(nc.vector, last, cols)
        for cols in halves:
            add_on_vector(last, cols)
            store(last, cols)
